import numpy as np
import ml_dtypes


def mxq(x, axis, fmt="e4m3"):
    dtype, down = {"e4m3": (ml_dtypes.float8_e4m3fn, 7), "e5m2": (ml_dtypes.float8_e5m2, 14)}[fmt]
    v = np.moveaxis(np.asarray(x, np.float32).astype(ml_dtypes.bfloat16).astype(np.float64), axis, -1)
    blocks = v.reshape(v.shape[:-1] + (-1, 32))
    amax = np.abs(blocks).max(-1, keepdims=True)
    byte = np.maximum(np.where(amax > 0, np.frexp(amax)[1] - 1 + 127, 0) - down, 1)
    scale = np.exp2(byte - 127.0)
    codes = (blocks / scale).astype(np.float32).astype(dtype).astype(np.float64)
    return np.moveaxis((codes * scale).reshape(v.shape), -1, axis)


WIDE = False


def mx_kscale(k):
    if not WIDE:
        return np.ones(k)
    levels = np.array([10, -10, 5, -5, 0])
    if k % 512:
        return np.exp2(np.random.permutation(np.resize(levels, k // 32))).repeat(32)
    a = np.empty((k // 512, 16))
    for p in range(k // 512):
        a[p, :8] = np.random.permutation(np.resize(levels, 8))
        for g in range(8):
            far = levels[np.abs(levels - a[p, g]) >= 10]
            a[p, g + 8] = far[np.random.randint(len(far))]
    return np.exp2(a.ravel()).repeat(32)


def f64(x):
    return np.asarray(x).astype(np.float64)


def striped8(idx):
    return np.concatenate([v.reshape(-1, 16).T for v in idx]).astype(np.uint16)


def unstriped8(offs):
    return np.stack([offs[16 * g:16 * g + 16].T.reshape(-1) for g in range(8)]).astype(np.int64)


def split(x):
    m, e = np.frexp(f64(x))
    hi = np.ldexp(np.trunc(16.0 * m) / 16.0, e)
    return hi, f64(x) - hi


K, M, T, S = 2048, 256, 2048, 512


def setup_inputs():
    n = np.random.standard_normal
    s = mx_kscale(K)[:, None]
    return {
        "xT": (n((K, T)) * s).astype(np.float32),
        "w": (n((K, M)) / np.sqrt(K) / s).astype(np.float32),
        "wgt": np.repeat(np.random.uniform(0.5, 2.0, (8, S)), 16, axis=0).astype(np.float32),
        "offs": striped8(np.stack([np.random.permutation(T)[:S] for _ in range(8)])),
    }


def reference(xT, w, wgt, offs):
    idx = unstriped8(offs)
    group = np.arange(K) % 512 // 64
    xg = f64(wgt)[np.arange(K) // 4 % 128] * f64(xT)[np.arange(K)[:, None], idx[group]]
    xT_ = mxq(xg, 0, "e4m3")
    w_hi, w_lo = split(w)
    w_hi_, w_lo_ = mxq(w_hi, 0, "e4m3"), mxq(w_lo, 0, "e4m3")
    y = xT_.T @ w_hi_ + xT_.T @ w_lo_
    return y

@@ -1,0 +1,162 @@
+from contextlib import ExitStack
+
+import concourse.mybir as mybir
+
+K, M, T, S = 2048, 256, 2048, 512
+FLOPS = 2 * 2 * K * M * S
+
+F32 = mybir.dt.float32
+BF16 = mybir.dt.bfloat16
+I32 = mybir.dt.int32
+U32 = mybir.dt.uint32
+U16 = mybir.dt.uint16
+U8 = mybir.dt.uint8
+FP8X4 = mybir.dt.float8_e4m3fn_x4
+MULT = mybir.AluOpType.mult
+SUB = mybir.AluOpType.subtract
+AND = mybir.AluOpType.bitwise_and
+
+P = 128
+PACK = 4
+K_PASS = P * PACK
+PASSES = K // K_PASS
+J_TILE = 128
+HI_MASK = -0x00100000
+
+
+def tile_list_heads_tm_hl_none_kernel(tc, xT, w, wgt, offs, out):
+    nc = tc.nc
+    with ExitStack() as ctx:
+        lists = ctx.enter_context(tc.tile_pool(name="lists", bufs=1))
+        keep = ctx.enter_context(tc.tile_pool(name="keep", bufs=1))
+        work = ctx.enter_context(tc.tile_pool(name="work", bufs=2))
+        psum = ctx.enter_context(tc.psum_pool(name="psum", bufs=1))
+
+        offs_sb = lists.tile([P, S // 16], U16, name="offs_sb")
+        nc.sync.dma_start(offs_sb[:], offs)
+
+        planes = [[keep.tile([P, T], F32, name=f"x_{a}_{i}") for i in range(PACK)] for a in range(PASSES)]
+        w_f32 = [keep.tile([P, PACK, M], F32, name=f"w_{a}") for a in range(PASSES)]
+        wgt_sb = keep.tile([P, S], F32, name="wgt_sb")
+
+        def load_w(a):
+            nc.sync.dma_start(w_f32[a][:], w[a * K_PASS : (a + 1) * K_PASS, :].rearrange("(p i) n -> p i n", i=PACK))
+
+        def load_plane(a, i):
+            rows = xT[a * K_PASS : (a + 1) * K_PASS, :].rearrange("(p i) t -> p i t", i=PACK)
+            nc.sync.dma_start(planes[a][i][:], rows[:, i, :])
+
+        load_w(0)
+        nc.sync.dma_start(wgt_sb[:], wgt)
+        load_w(1)
+        load_plane(0, 0)
+        load_w(2)
+        load_w(3)
+        for a in range(PASSES):
+            for i in range(PACK):
+                if (a, i) != (0, 0):
+                    load_plane(a, i)
+
+        x_codes = [keep.tile([P, S], U32, name=f"xc_{a}", align_bytes=64) for a in range(PASSES)]
+        x_scales = [keep.tile([P, S], U8, name=f"xs_{a}", align_bytes=64) for a in range(PASSES)]
+        w_codes = [keep.tile([P, 2 * M], U32, name=f"wc_{a}", align_bytes=64) for a in range(PASSES)]
+        w_scales = [keep.tile([P, 2 * M], U8, name=f"ws_{a}", align_bytes=64) for a in range(PASSES)]
+        sums = [[(slice(0, M), psum.tile([J_TILE, M], F32, name=f"sum_{j}"))] for j in range(3)]
+        sums.append([(slice(h, h + 128), psum.tile([J_TILE, 128], F32, name=f"sum_3_{h}")) for h in (0, 128)])
+
+        def round_to(columns, planes_f32):
+            nc.scalar.copy(
+                columns.rearrange("p (c m) i -> p c i m", m=4), planes_f32.rearrange("p i (c m) -> p c i m", m=4)
+            )
+
+        def split_w(a):
+            hi = work.tile([P, PACK, M], F32, name="w_hi")
+            lo = work.tile([P, PACK, M], F32, name="w_lo")
+            rounded = work.tile([P, 2 * M, PACK], BF16, name="w_rounded", align_bytes=64)
+            nc.vector.tensor_scalar(hi[:].bitcast(I32), w_f32[a][:].bitcast(I32), HI_MASK, None, AND)
+            nc.vector.tensor_tensor(lo[:], w_f32[a][:], hi[:], SUB)
+            round_to(rounded[:, :M, :], hi[:])
+            round_to(rounded[:, M:, :], lo[:])
+            return rounded
+
+        def quantise_w(a, rounded):
+            nc.vector.quantize_mx(
+                out=w_codes[a][:].bitcast(FP8X4), scales=w_scales[a][:], in_=rounded[:].rearrange("p n i -> p (n i)")
+            )
+
+        def pick(a, i, j0, width, picked):
+            nc.vector.tensor_tensor(
+                picked,
+                planes[a][i][:].indirect(offs_sb[:, j0 // 16 : (j0 + width) // 16]),
+                wgt_sb[:, j0 : j0 + width],
+                MULT,
+            )
+
+        def quantise(a, j0, width, rounded):
+            nc.vector.quantize_mx(
+                out=x_codes[a][:, j0 : j0 + width].bitcast(FP8X4), scales=x_scales[a][:, j0 : j0 + width], in_=rounded
+            )
+
+        def multiply(a, j):
+            cols = slice(j * J_TILE, (j + 1) * J_TILE)
+            for n_cols, total in sums[j]:
+                for part in range(2):
+                    w_cols = slice(part * M + n_cols.start, part * M + n_cols.stop)
+                    nc.tensor.matmul_mx(
+                        out=total[:],
+                        lhsT=x_codes[a][:, cols].bitcast(FP8X4),
+                        lhsT_scale=x_scales[a][:, cols],
+                        rhs=w_codes[a][:, w_cols].bitcast(FP8X4),
+                        rhs_scale=w_scales[a][:, w_cols],
+                        start=(a == 0 and part == 0),
+                        stop=(a == PASSES - 1 and part == 1),
+                    )
+
+        def finish(a, rounded):
+            quantise(a, 0, S, rounded[:].rearrange("p j i -> p (j i)"))
+            for j in range(S // J_TILE):
+                multiply(a, j)
+
+        w_rounded = [split_w(0), split_w(1)]
+        waiting = None
+        for a in range(PASSES - 1):
+            picked = work.tile([P, PACK, S], F32, name="picked")
+            for i in range(PACK):
+                for j0 in (0, 256):
+                    pick(a, i, j0, 256, picked[:, i, j0 : j0 + 256])
+                if a == 0 and i == 0:
+                    for b in range(2):
+                        quantise_w(b, w_rounded[b])
+                    w_rounded = [split_w(2), split_w(3)]
+                if a == 0 and i == 1:
+                    for b in range(2):
+                        quantise_w(b + 2, w_rounded[b])
+                if a > 0 and i == 1:
+                    finish(a - 1, waiting)
+            waiting = work.tile([P, S, PACK], BF16, name="rounded", align_bytes=64)
+            for j0 in (0, 256):
+                round_to(waiting[:, j0 : j0 + 256, :], picked[:, :, j0 : j0 + 256])
+
+        a = PASSES - 1
+        rounded_last = keep.tile([P, S, PACK], BF16, name="rounded_last", align_bytes=64)
+        for i in range(PACK):
+            width = 256 if i < PACK - 1 else J_TILE
+            picked_last = keep.tile([P, S], F32, name=f"picked_last_{i}")
+            for j0 in range(0, S, width):
+                pick(a, i, j0, width, picked_last[:, j0 : j0 + width])
+                nc.scalar.copy(rounded_last[:, j0 : j0 + width, i], picked_last[:, j0 : j0 + width])
+            if i == 2:
+                finish(a - 1, waiting)
+        for j in range(S // J_TILE):
+            j0 = j * J_TILE
+            quantise(a, j0, J_TILE, rounded_last[:, j0 : j0 + J_TILE, :].rearrange("p j i -> p (j i)"))
+            multiply(a, j)
+
+        for j in range(S // J_TILE):
+            result = keep.tile([J_TILE, M], F32, name=f"result_{j}")
+            for n_cols, total in sums[j]:
+                if j == 1 or (j == 3 and n_cols.start == 0):
+                    nc.vector.tensor_copy(result[:, n_cols], total[:])
+                else:
+                    nc.scalar.copy(result[:, n_cols], total[:])
+            nc.sync.dma_start(out[j * J_TILE : (j + 1) * J_TILE, :], result[:])

@@ -35,9 +35,21 @@ def tile_list_heads_tm_hl_none_kernel(tc, xT, w, wgt, offs, out):
         offs_sb = lists.tile([P, S // 16], U16, name="offs_sb")
         nc.sync.dma_start(offs_sb[:], offs)
 
-        planes = [[keep.tile([P, T], F32, name=f"x_{a}_{i}") for i in range(PACK)] for a in range(PASSES)]
+        planes = [[keep.tile([P, T], F32, name=f"x_{a}_{i}", align_bytes=64) for i in range(PACK)] for a in range(PASSES)]
         w_f32 = [keep.tile([P, PACK, M], F32, name=f"w_{a}") for a in range(PASSES)]
-        wgt_sb = keep.tile([P, S], F32, name="wgt_sb")
+        wgt_sb = keep.tile([P, S], F32, name="wgt_sb", align_bytes=64)
+
+        def load_wgt():
+            rows = keep.tile([P, 32], F32, name="wgt_rows", align_bytes=64)
+            turned = keep.tile([P, 32], F32, name="wgt_turned", align_bytes=64)
+            spread = keep.tile([P, S], F32, name="wgt_spread", align_bytes=64)
+            nc.sync.dma_start(rows[:], wgt.rearrange("(g s) (r c) -> g s r c", s=16, c=32)[:, 0, :, :])
+            nc.vector.transpose(turned[:], rows[:])
+            nc.scalar.copy(
+                spread[:].rearrange("p (r h s) -> p r h s", h=2, s=16),
+                turned[:].rearrange("p (h r) -> p r h", h=2).unsqueeze(3).to_broadcast([P, 16, 2, 16]),
+            )
+            nc.vector.transpose(wgt_sb[:], spread[:])
 
         def load_w(a):
             nc.sync.dma_start(w_f32[a][:], w[a * K_PASS : (a + 1) * K_PASS, :].rearrange("(p i) n -> p i n", i=PACK))
@@ -47,7 +59,7 @@ def tile_list_heads_tm_hl_none_kernel(tc, xT, w, wgt, offs, out):
             nc.sync.dma_start(planes[a][i][:], rows[:, i, :])
 
         load_w(0)
-        nc.sync.dma_start(wgt_sb[:], wgt)
+        load_wgt()
         load_w(1)
         load_plane(0, 0)
         load_w(2)
@@ -57,7 +69,7 @@ def tile_list_heads_tm_hl_none_kernel(tc, xT, w, wgt, offs, out):
                 if (a, i) != (0, 0):
                     load_plane(a, i)
 
-        x_codes = [keep.tile([P, S], U32, name=f"xc_{a}", align_bytes=64) for a in range(PASSES)]
+        x_codes = {a: keep.tile([P, S], U32, name=f"xc_{a}", align_bytes=64) for a in (0, 3)}
         x_scales = [keep.tile([P, S], U8, name=f"xs_{a}", align_bytes=64) for a in range(PASSES)]
         w_codes = [keep.tile([P, 2 * M], U32, name=f"wc_{a}", align_bytes=64) for a in range(PASSES)]
         w_scales = [keep.tile([P, 2 * M], U8, name=f"ws_{a}", align_bytes=64) for a in range(PASSES)]
@@ -118,12 +130,11 @@ def tile_list_heads_tm_hl_none_kernel(tc, xT, w, wgt, offs, out):
                 multiply(a, j)
 
         w_rounded = [split_w(0), split_w(1)]
-        waiting = None
+        waiting = []
         for a in range(PASSES - 1):
             picked = work.tile([P, PACK, S], F32, name="picked")
             for i in range(PACK):
-                for j0 in (0, 256):
-                    pick(a, i, j0, 256, picked[:, i, j0 : j0 + 256])
+                pick(a, i, 0, S, picked[:, i, :])
                 if a == 0 and i == 0:
                     for b in range(2):
                         quantise_w(b, w_rounded[b])
@@ -131,32 +142,68 @@ def tile_list_heads_tm_hl_none_kernel(tc, xT, w, wgt, offs, out):
                 if a == 0 and i == 1:
                     for b in range(2):
                         quantise_w(b + 2, w_rounded[b])
-                if a > 0 and i == 1:
-                    finish(a - 1, waiting)
-            waiting = work.tile([P, S, PACK], BF16, name="rounded", align_bytes=64)
+                if a == 1 and i == 1:
+                    finish(0, waiting[0])
+            rounded = keep.tile([P, S, PACK], BF16, name=f"rounded_{a}", align_bytes=64)
             for j0 in (0, 256):
-                round_to(waiting[:, j0 : j0 + 256, :], picked[:, :, j0 : j0 + 256])
+                round_to(rounded[:, j0 : j0 + 256, :], picked[:, :, j0 : j0 + 256])
+            waiting.append(rounded)
 
         a = PASSES - 1
-        rounded_last = keep.tile([P, S, PACK], BF16, name="rounded_last", align_bytes=64)
-        for i in range(PACK):
-            width = 256 if i < PACK - 1 else J_TILE
-            picked_last = keep.tile([P, S], F32, name=f"picked_last_{i}")
-            for j0 in range(0, S, width):
-                pick(a, i, j0, width, picked_last[:, j0 : j0 + width])
-                nc.scalar.copy(rounded_last[:, j0 : j0 + width, i], picked_last[:, j0 : j0 + width])
-            if i == 2:
-                finish(a - 1, waiting)
-        for j in range(S // J_TILE):
+        tiles = S // J_TILE
+        vector_tile = 1
+        rounded_last = [keep.tile([P, J_TILE, PACK], BF16, name=f"rounded_last_{j}", align_bytes=64) for j in range(tiles)]
+        picked = work.tile([P, PACK, S], F32, name="picked")
+
+        def round_last(j, i0, i1):
+            source = picked[:, i0:i1, j * J_TILE : (j + 1) * J_TILE].rearrange("p i j -> p j i")
+            if j == vector_tile:
+                nc.vector.tensor_copy(rounded_last[j][:, :, i0:i1], source)
+            else:
+                nc.scalar.copy(rounded_last[j][:, :, i0:i1], source)
+
+        for i in range(PACK - 1):
+            for j0 in (0, 256):
+                pick(a, i, j0, 256, picked[:, i, j0 : j0 + 256])
+                for j in (j0 // J_TILE, j0 // J_TILE + 1):
+                    if j != vector_tile:
+                        round_last(j, i, i + 1)
+            if i > 0:
+                x_codes.setdefault(i, keep.tile([P, S], U32, name=f"x_3_{i}", align_bytes=64))
+                finish(i, waiting[i])
+            if i == 1:
+                round_last(vector_tile, 0, 2)
+
+        results = work.tile([J_TILE, tiles, M], F32, name="w_hi")
+
+        def pick_last(j):
             j0 = j * J_TILE
-            quantise(a, j0, J_TILE, rounded_last[:, j0 : j0 + J_TILE, :].rearrange("p j i -> p (j i)"))
+            pick(a, PACK - 1, j0, J_TILE, picked[:, PACK - 1, j0 : j0 + J_TILE])
+            if j != vector_tile:
+                round_last(j, PACK - 1, PACK)
+
+        def finish_last(j):
+            quantise(a, j * J_TILE, J_TILE, rounded_last[j][:].rearrange("p j i -> p (j i)"))
             multiply(a, j)
 
-        for j in range(S // J_TILE):
-            result = keep.tile([J_TILE, M], F32, name=f"result_{j}")
+        def store(j):
             for n_cols, total in sums[j]:
                 if j == 1 or (j == 3 and n_cols.start == 0):
-                    nc.vector.tensor_copy(result[:, n_cols], total[:])
+                    nc.vector.tensor_copy(results[:, j, n_cols], total[:])
                 else:
-                    nc.scalar.copy(result[:, n_cols], total[:])
-            nc.sync.dma_start(out[j * J_TILE : (j + 1) * J_TILE, :], result[:])
+                    nc.scalar.copy(results[:, j, n_cols], total[:])
+            nc.sync.dma_start(out[j * J_TILE : (j + 1) * J_TILE, :], results[:, j, :])
+
+        pick_last(0)
+        pick_last(1)
+        pick_last(2)
+        pick_last(3)
+        round_last(vector_tile, 2, PACK)
+        finish_last(0)
+        finish_last(1)
+        finish_last(2)
+        finish_last(3)
+        store(0)
+        store(1)
+        store(2)
+        store(3)

@@ -21,6 +21,7 @@ PACK = 4
 K_PASS = P * PACK
 PASSES = K // K_PASS
 J_TILE = 128
+PAIRS = ((0, 2), (1, 0), (1, 2))
 HI_MASK = -0x00100000
 
 
@@ -35,8 +36,9 @@ def tile_list_heads_tm_hl_none_kernel(tc, xT, w, wgt, offs, out):
         offs_sb = lists.tile([P, S // 16], U16, name="offs_sb")
         nc.sync.dma_start(offs_sb[:], offs)
 
-        planes = [[keep.tile([P, T], F32, name=f"x_{a}_{i}", align_bytes=64) for i in range(PACK)] for a in range(PASSES)]
-        w_f32 = [keep.tile([P, PACK, M], F32, name=f"w_{a}") for a in range(PASSES)]
+        planes = {}
+        w_pairs = [keep.tile([P, 2, PACK, M], F32, name=f"w_{h}") for h in range(PASSES // 2)]
+        w_f32 = [w_pairs[a // 2][:, a % 2] for a in range(PASSES)]
         wgt_sb = keep.tile([P, S], F32, name="wgt_sb", align_bytes=64)
 
         def load_wgt():
@@ -51,23 +53,24 @@ def tile_list_heads_tm_hl_none_kernel(tc, xT, w, wgt, offs, out):
             )
             nc.vector.transpose(wgt_sb[:], spread[:])
 
-        def load_w(a):
-            nc.sync.dma_start(w_f32[a][:], w[a * K_PASS : (a + 1) * K_PASS, :].rearrange("(p i) n -> p i n", i=PACK))
+        def load_w(h):
+            rows = w[2 * h * K_PASS : 2 * (h + 1) * K_PASS, :]
+            nc.sync.dma_start(w_pairs[h][:], rows.rearrange("(a p i) n -> p a i n", a=2, i=PACK))
 
-        def load_plane(a, i):
-            rows = xT[a * K_PASS : (a + 1) * K_PASS, :].rearrange("(p i) t -> p i t", i=PACK)
-            nc.sync.dma_start(planes[a][i][:], rows[:, i, :])
+        def load_planes(a, i, count):
+            tile = keep.tile([P, count * T], F32, name=f"x_{a}_{i}", align_bytes=64)
+            rows = xT[a * K_PASS : (a + 1) * K_PASS, :].rearrange("(p i) t -> p (i t)", i=PACK)
+            nc.sync.dma_start(tile[:], rows[:, i * T : (i + count) * T])
+            planes.setdefault((a, i), tile)
 
         load_w(0)
         load_wgt()
+        load_planes(0, 0, 1)
         load_w(1)
-        load_plane(0, 0)
-        load_w(2)
-        load_w(3)
         for a in range(PASSES):
             for i in range(PACK):
-                if (a, i) != (0, 0):
-                    load_plane(a, i)
+                if (a, i) != (0, 0) and (a, i - 1) not in PAIRS:
+                    load_planes(a, i, 2 if (a, i) in PAIRS else 1)
 
         x_codes = {a: keep.tile([P, S], U32, name=f"xc_{a}", align_bytes=64) for a in (0, 3)}
         x_scales = [keep.tile([P, S], U8, name=f"xs_{a}", align_bytes=64) for a in range(PASSES)]
@@ -85,8 +88,8 @@ def tile_list_heads_tm_hl_none_kernel(tc, xT, w, wgt, offs, out):
             hi = work.tile([P, PACK, M], F32, name="w_hi")
             lo = work.tile([P, PACK, M], F32, name="w_lo")
             rounded = work.tile([P, 2 * M, PACK], BF16, name="w_rounded", align_bytes=64)
-            nc.vector.tensor_scalar(hi[:].bitcast(I32), w_f32[a][:].bitcast(I32), HI_MASK, None, AND)
-            nc.vector.tensor_tensor(lo[:], w_f32[a][:], hi[:], SUB)
+            nc.vector.tensor_scalar(hi[:].bitcast(I32), w_f32[a].bitcast(I32), HI_MASK, None, AND)
+            nc.vector.tensor_tensor(lo[:], w_f32[a], hi[:], SUB)
             round_to(rounded[:, :M, :], hi[:])
             round_to(rounded[:, M:, :], lo[:])
             return rounded
@@ -99,7 +102,7 @@ def tile_list_heads_tm_hl_none_kernel(tc, xT, w, wgt, offs, out):
         def pick(a, i, j0, width, picked):
             nc.vector.tensor_tensor(
                 picked,
-                planes[a][i][:].indirect(offs_sb[:, j0 // 16 : (j0 + width) // 16]),
+                planes[a, i][:].indirect(offs_sb[:, j0 // 16 : (j0 + width) // 16]),
                 wgt_sb[:, j0 : j0 + width],
                 MULT,
             )
@@ -134,7 +137,14 @@ def tile_list_heads_tm_hl_none_kernel(tc, xT, w, wgt, offs, out):
         for a in range(PASSES - 1):
             picked = work.tile([P, PACK, S], F32, name="picked")
             for i in range(PACK):
-                pick(a, i, 0, S, picked[:, i, :])
+                if (a, i) in PAIRS:
+                    second = work.tile([P, T], F32, name="second")
+                    nc.scalar.copy(second[:], planes[a, i][:, T:])
+                    planes.setdefault((a, i + 1), second)
+                    for j0 in (0, 256):
+                        pick(a, i, j0, 256, picked[:, i, j0 : j0 + 256])
+                else:
+                    pick(a, i, 0, S, picked[:, i, :])
                 if a == 0 and i == 0:
                     for b in range(2):
                         quantise_w(b, w_rounded[b])

@@ -34,7 +34,6 @@ def tile_list_heads_tm_hl_none_kernel(tc, xT, w, wgt, offs, out):
         psum = ctx.enter_context(tc.psum_pool(name="psum", bufs=1))
 
         offs_sb = lists.tile([P, S // 16], U16, name="offs_sb")
-        nc.sync.dma_start(offs_sb[:], offs)
 
         planes = {}
         w_pairs = [keep.tile([P, 2, PACK, M], F32, name=f"w_{h}") for h in range(PASSES // 2)]
@@ -45,7 +44,7 @@ def tile_list_heads_tm_hl_none_kernel(tc, xT, w, wgt, offs, out):
             rows = keep.tile([P, 32], F32, name="wgt_rows", align_bytes=64)
             turned = keep.tile([P, 32], F32, name="wgt_turned", align_bytes=64)
             spread = keep.tile([P, S], F32, name="wgt_spread", align_bytes=64)
-            nc.sync.dma_start(rows[:], wgt.rearrange("(g s) (r c) -> g s r c", s=16, c=32)[:, 0, :, :])
+            nc.sync.dma_start(rows[:], wgt.rearrange("p (h c) -> (p h) c", h=2)[0 : 2 * P : 17, :].rearrange("u (r c) -> u r c", c=32))
             nc.vector.transpose(turned[:], rows[:])
             nc.scalar.copy(
                 spread[:].rearrange("p (r h s) -> p r h s", h=2, s=16),
@@ -64,6 +63,7 @@ def tile_list_heads_tm_hl_none_kernel(tc, xT, w, wgt, offs, out):
             planes.setdefault((a, i), tile)
 
         load_w(0)
+        nc.sync.dma_start(offs_sb[:], offs)
         load_wgt()
         load_planes(0, 0, 1)
         load_w(1)
@@ -72,7 +72,7 @@ def tile_list_heads_tm_hl_none_kernel(tc, xT, w, wgt, offs, out):
                 if (a, i) != (0, 0) and (a, i - 1) not in PAIRS:
                     load_planes(a, i, 2 if (a, i) in PAIRS else 1)
 
-        x_codes = {a: keep.tile([P, S], U32, name=f"xc_{a}", align_bytes=64) for a in (0, 3)}
+        x_codes = {a: keep.tile([P, S], U32, name=f"xc_{a}", align_bytes=64) for a in (0, 2, 3)}
         x_scales = [keep.tile([P, S], U8, name=f"xs_{a}", align_bytes=64) for a in range(PASSES)]
         w_codes = [keep.tile([P, 2 * M], U32, name=f"wc_{a}", align_bytes=64) for a in range(PASSES)]
         w_scales = [keep.tile([P, 2 * M], U8, name=f"ws_{a}", align_bytes=64) for a in range(PASSES)]
@@ -107,9 +107,16 @@ def tile_list_heads_tm_hl_none_kernel(tc, xT, w, wgt, offs, out):
                 MULT,
             )
 
+        def codes_of(a, j0, width):
+            if a == 1:
+                return late_codes[j0 // 256][:, j0 % 256 : j0 % 256 + width]
+            return x_codes[a][:, j0 : j0 + width]
+
+        late_codes = []
+
         def quantise(a, j0, width, rounded):
             nc.vector.quantize_mx(
-                out=x_codes[a][:, j0 : j0 + width].bitcast(FP8X4), scales=x_scales[a][:, j0 : j0 + width], in_=rounded
+                out=codes_of(a, j0, width).bitcast(FP8X4), scales=x_scales[a][:, j0 : j0 + width], in_=rounded
             )
 
         def multiply(a, j):
@@ -119,7 +126,7 @@ def tile_list_heads_tm_hl_none_kernel(tc, xT, w, wgt, offs, out):
                     w_cols = slice(part * M + n_cols.start, part * M + n_cols.stop)
                     nc.tensor.matmul_mx(
                         out=total[:],
-                        lhsT=x_codes[a][:, cols].bitcast(FP8X4),
+                        lhsT=codes_of(a, cols.start, J_TILE).bitcast(FP8X4),
                         lhsT_scale=x_scales[a][:, cols],
                         rhs=w_codes[a][:, w_cols].bitcast(FP8X4),
                         rhs_scale=w_scales[a][:, w_cols],
@@ -161,7 +168,7 @@ def tile_list_heads_tm_hl_none_kernel(tc, xT, w, wgt, offs, out):
 
         a = PASSES - 1
         tiles = S // J_TILE
-        vector_tile = 1
+        vector_tile = 3
         rounded_last = [keep.tile([P, J_TILE, PACK], BF16, name=f"rounded_last_{j}", align_bytes=64) for j in range(tiles)]
         picked = work.tile([P, PACK, S], F32, name="picked")
 
@@ -179,8 +186,14 @@ def tile_list_heads_tm_hl_none_kernel(tc, xT, w, wgt, offs, out):
                     if j != vector_tile:
                         round_last(j, i, i + 1)
             if i > 0:
-                x_codes.setdefault(i, keep.tile([P, S], U32, name=f"x_3_{i}", align_bytes=64))
-                finish(i, waiting[i])
+                late_codes.append(keep.tile([P, 256], U32, name=f"x_3_{i}", align_bytes=64))
+                j0 = (i - 1) * 256
+                quantise(1, j0, 256, waiting[1][:, j0 : j0 + 256, :].rearrange("p j i -> p (j i)"))
+                for j in (j0 // J_TILE, j0 // J_TILE + 1):
+                    multiply(1, j)
+                    multiply(2, j)
+            if i == 0:
+                quantise(2, 0, S, waiting[2][:].rearrange("p j i -> p (j i)"))
             if i == 1:
                 round_last(vector_tile, 0, 2)
 
@@ -198,7 +211,7 @@ def tile_list_heads_tm_hl_none_kernel(tc, xT, w, wgt, offs, out):
 
         def store(j):
             for n_cols, total in sums[j]:
-                if j == 1 or (j == 3 and n_cols.start == 0):
+                if j == 2 or (j == 3 and n_cols.start > 0):
                     nc.vector.tensor_copy(results[:, j, n_cols], total[:])
                 else:
                     nc.scalar.copy(results[:, j, n_cols], total[:])
@@ -208,8 +221,8 @@ def tile_list_heads_tm_hl_none_kernel(tc, xT, w, wgt, offs, out):
         pick_last(1)
         pick_last(2)
         pick_last(3)
-        round_last(vector_tile, 2, PACK)
         finish_last(0)
+        round_last(vector_tile, 2, PACK)
         finish_last(1)
         finish_last(2)
         finish_last(3)

@@ -21,7 +21,7 @@ PACK = 4
 K_PASS = P * PACK
 PASSES = K // K_PASS
 J_TILE = 128
-PAIRS = ((0, 2), (1, 0), (1, 2))
+PAIRS = ()
 HI_MASK = -0x00100000
 
 

@@ -72,7 +72,7 @@ def tile_list_heads_tm_hl_none_kernel(tc, xT, w, wgt, offs, out):
                 if (a, i) != (0, 0) and (a, i - 1) not in PAIRS:
                     load_planes(a, i, 2 if (a, i) in PAIRS else 1)
 
-        x_codes = {a: keep.tile([P, S], U32, name=f"xc_{a}", align_bytes=64) for a in (0, 2, 3)}
+        x_codes = {a: keep.tile([P, S], U32, name=f"xc_{a}", align_bytes=64) for a in (0, 1, 3)}
         x_scales = [keep.tile([P, S], U8, name=f"xs_{a}", align_bytes=64) for a in range(PASSES)]
         w_codes = [keep.tile([P, 2 * M], U32, name=f"wc_{a}", align_bytes=64) for a in range(PASSES)]
         w_scales = [keep.tile([P, 2 * M], U8, name=f"ws_{a}", align_bytes=64) for a in range(PASSES)]
@@ -108,7 +108,7 @@ def tile_list_heads_tm_hl_none_kernel(tc, xT, w, wgt, offs, out):
             )
 
         def codes_of(a, j0, width):
-            if a == 1:
+            if a == 2:
                 return late_codes[j0 // 256][:, j0 % 256 : j0 % 256 + width]
             return x_codes[a][:, j0 : j0 + width]
 
@@ -161,6 +161,8 @@ def tile_list_heads_tm_hl_none_kernel(tc, xT, w, wgt, offs, out):
                         quantise_w(b + 2, w_rounded[b])
                 if a == 1 and i == 1:
                     finish(0, waiting[0])
+                if a == 2 and i == 1:
+                    quantise(1, 0, S, waiting[1][:].rearrange("p j i -> p (j i)"))
             rounded = keep.tile([P, S, PACK], BF16, name=f"rounded_{a}", align_bytes=64)
             for j0 in (0, 256):
                 round_to(rounded[:, j0 : j0 + 256, :], picked[:, :, j0 : j0 + 256])
@@ -183,17 +185,15 @@ def tile_list_heads_tm_hl_none_kernel(tc, xT, w, wgt, offs, out):
             for j0 in (0, 256):
                 pick(a, i, j0, 256, picked[:, i, j0 : j0 + 256])
                 for j in (j0 // J_TILE, j0 // J_TILE + 1):
-                    if j != vector_tile:
-                        round_last(j, i, i + 1)
+                    if j != vector_tile and i > 0:
+                        round_last(j, 0 if i == 1 else i, i + 1)
             if i > 0:
                 late_codes.append(keep.tile([P, 256], U32, name=f"x_3_{i}", align_bytes=64))
                 j0 = (i - 1) * 256
-                quantise(1, j0, 256, waiting[1][:, j0 : j0 + 256, :].rearrange("p j i -> p (j i)"))
+                quantise(2, j0, 256, waiting[2][:, j0 : j0 + 256, :].rearrange("p j i -> p (j i)"))
                 for j in (j0 // J_TILE, j0 // J_TILE + 1):
-                    multiply(1, j)
                     multiply(2, j)
-            if i == 0:
-                quantise(2, 0, S, waiting[2][:].rearrange("p j i -> p (j i)"))
+                    multiply(1, j)
             if i == 1:
                 round_last(vector_tile, 0, 2)
 

@@ -21,7 +21,7 @@ PACK = 4
 K_PASS = P * PACK
 PASSES = K // K_PASS
 J_TILE = 128
-PAIRS = ()
+PAIRS = ((0, 2), (1, 0), (1, 2))
 HI_MASK = -0x00100000
 
 
@@ -65,7 +65,7 @@ def tile_list_heads_tm_hl_none_kernel(tc, xT, w, wgt, offs, out):
         load_w(0)
         nc.sync.dma_start(offs_sb[:], offs)
         load_wgt()
-        load_planes(0, 0, 1)
+        load_planes(0, 0, 2 if (0, 0) in PAIRS else 1)
         load_w(1)
         for a in range(PASSES):
             for i in range(PACK):
@@ -141,6 +141,14 @@ def tile_list_heads_tm_hl_none_kernel(tc, xT, w, wgt, offs, out):
 
         w_rounded = [split_w(0), split_w(1)]
         waiting = []
+        picked_before = None
+
+        def round_pass(a, values):
+            rounded = keep.tile([P, S, PACK], BF16, name=f"rounded_{a}", align_bytes=64)
+            for j0 in range(0, S, J_TILE):
+                round_to(rounded[:, j0 : j0 + J_TILE, :], values[:, :, j0 : j0 + J_TILE])
+            waiting.append(rounded)
+
         for a in range(PASSES - 1):
             picked = work.tile([P, PACK, S], F32, name="picked")
             for i in range(PACK):
@@ -159,14 +167,14 @@ def tile_list_heads_tm_hl_none_kernel(tc, xT, w, wgt, offs, out):
                 if a == 0 and i == 1:
                     for b in range(2):
                         quantise_w(b + 2, w_rounded[b])
-                if a == 1 and i == 1:
+                if a > 0 and i == 2:
+                    round_pass(a - 1, picked_before)
+                if a == 2 and i == 0:
                     finish(0, waiting[0])
-                if a == 2 and i == 1:
+                if a == 2 and i == 3:
                     quantise(1, 0, S, waiting[1][:].rearrange("p j i -> p (j i)"))
-            rounded = keep.tile([P, S, PACK], BF16, name=f"rounded_{a}", align_bytes=64)
-            for j0 in (0, 256):
-                round_to(rounded[:, j0 : j0 + 256, :], picked[:, :, j0 : j0 + 256])
-            waiting.append(rounded)
+            picked_before = picked
+        round_pass(PASSES - 2, picked_before)
 
         a = PASSES - 1
         tiles = S // J_TILE

@@ -36,7 +36,7 @@ def tile_list_heads_tm_hl_none_kernel(tc, xT, w, wgt, offs, out):
         offs_sb = lists.tile([P, S // 16], U16, name="offs_sb")
 
         planes = {}
-        w_pairs = [keep.tile([P, 2, PACK, M], F32, name=f"w_{h}") for h in range(PASSES // 2)]
+        w_pairs = [keep.tile([P, 2, PACK, M], F32, name=f"w_{h}", align_bytes=256) for h in range(PASSES // 2)]
         w_f32 = [w_pairs[a // 2][:, a % 2] for a in range(PASSES)]
         wgt_sb = keep.tile([P, S], F32, name="wgt_sb", align_bytes=64)
 
@@ -57,7 +57,7 @@ def tile_list_heads_tm_hl_none_kernel(tc, xT, w, wgt, offs, out):
             nc.sync.dma_start(w_pairs[h][:], rows.rearrange("(a p i) n -> p a i n", a=2, i=PACK))
 
         def load_planes(a, i, count):
-            tile = keep.tile([P, count * T], F32, name=f"x_{a}_{i}", align_bytes=64)
+            tile = keep.tile([P, count * T], F32, name=f"x_{a}_{i}", align_bytes=256)
             rows = xT[a * K_PASS : (a + 1) * K_PASS, :].rearrange("(p i) t -> p (i t)", i=PACK)
             nc.sync.dma_start(tile[:], rows[:, i * T : (i + count) * T])
             planes.setdefault((a, i), tile)
@@ -85,7 +85,7 @@ def tile_list_heads_tm_hl_none_kernel(tc, xT, w, wgt, offs, out):
             )
 
         def split_w(a):
-            hi = work.tile([P, PACK, M], F32, name="w_hi")
+            hi = work.tile([P, PACK, M], F32, name="w_hi", align_bytes=256)
             lo = work.tile([P, PACK, M], F32, name="w_lo")
             rounded = work.tile([P, 2 * M, PACK], BF16, name="w_rounded", align_bytes=64)
             nc.vector.tensor_scalar(hi[:].bitcast(I32), w_f32[a].bitcast(I32), HI_MASK, None, AND)
@@ -144,7 +144,7 @@ def tile_list_heads_tm_hl_none_kernel(tc, xT, w, wgt, offs, out):
         picked_before = None
 
         def round_pass(a, values):
-            rounded = keep.tile([P, S, PACK], BF16, name=f"rounded_{a}", align_bytes=64)
+            rounded = keep.tile([P, S, PACK], BF16, name=f"rounded_{a % 2}", align_bytes=64)
             for j0 in range(0, S, J_TILE):
                 round_to(rounded[:, j0 : j0 + J_TILE, :], values[:, :, j0 : j0 + J_TILE])
             waiting.append(rounded)
@@ -196,7 +196,7 @@ def tile_list_heads_tm_hl_none_kernel(tc, xT, w, wgt, offs, out):
                     if j != vector_tile and i > 0:
                         round_last(j, 0 if i == 1 else i, i + 1)
             if i > 0:
-                late_codes.append(keep.tile([P, 256], U32, name=f"x_3_{i}", align_bytes=64))
+                late_codes.append(keep.tile([P, 256], U32, name=f"x_3_{i}", align_bytes=256))
                 j0 = (i - 1) * 256
                 quantise(2, j0, 256, waiting[2][:, j0 : j0 + 256, :].rearrange("p j i -> p (j i)"))
                 for j in (j0 // J_TILE, j0 // J_TILE + 1):
@@ -205,7 +205,7 @@ def tile_list_heads_tm_hl_none_kernel(tc, xT, w, wgt, offs, out):
             if i == 1:
                 round_last(vector_tile, 0, 2)
 
-        results = work.tile([J_TILE, tiles, M], F32, name="w_hi")
+        results = work.tile([J_TILE, tiles, M], F32, name="w_hi", align_bytes=256)
 
         def pick_last(j):
             j0 = j * J_TILE

@@ -20,9 +20,15 @@ P = 128
 PACK = 4
 K_PASS = P * PACK
 PASSES = K // K_PASS
+LAST = PASSES - 1
 J_TILE = 128
-PAIRS = ((0, 2), (1, 0), (1, 2))
+TILES = S // J_TILE
+HALF = S // 2
+LIST_ROWS = 16
 HI_MASK = -0x00100000
+MX_ALIGN = 64
+DMA_ALIGN = 256
+SCALAR_COLUMNS = (128, 128, 96, 64)
 
 
 def tile_list_heads_tm_hl_none_kernel(tc, xT, w, wgt, offs, out):
@@ -33,65 +39,72 @@ def tile_list_heads_tm_hl_none_kernel(tc, xT, w, wgt, offs, out):
         work = ctx.enter_context(tc.tile_pool(name="work", bufs=2))
         psum = ctx.enter_context(tc.psum_pool(name="psum", bufs=1))
 
-        offs_sb = lists.tile([P, S // 16], U16, name="offs_sb")
-
-        planes = {}
-        w_pairs = [keep.tile([P, 2, PACK, M], F32, name=f"w_{h}", align_bytes=256) for h in range(PASSES // 2)]
+        offs_sb = lists.tile([P, S // LIST_ROWS], U16, name="offs_sb", align_bytes=DMA_ALIGN)
+        w_pairs = [keep.tile([P, 2, PACK, M], F32, name=f"w_{h}", align_bytes=DMA_ALIGN) for h in range(PASSES // 2)]
         w_f32 = [w_pairs[a // 2][:, a % 2] for a in range(PASSES)]
-        wgt_sb = keep.tile([P, S], F32, name="wgt_sb", align_bytes=64)
+        wgt_sb = keep.tile([P, S], F32, name="wgt_sb", align_bytes=MX_ALIGN)
+        planes = {}
 
-        def load_wgt():
-            rows = keep.tile([P, 32], F32, name="wgt_rows", align_bytes=64)
-            turned = keep.tile([P, 32], F32, name="wgt_turned", align_bytes=64)
-            spread = keep.tile([P, S], F32, name="wgt_spread", align_bytes=64)
-            nc.sync.dma_start(rows[:], wgt.rearrange("p (h c) -> (p h) c", h=2)[0 : 2 * P : 17, :].rearrange("u (r c) -> u r c", c=32))
-            nc.vector.transpose(turned[:], rows[:])
-            nc.scalar.copy(
-                spread[:].rearrange("p (r h s) -> p r h s", h=2, s=16),
-                turned[:].rearrange("p (h r) -> p r h", h=2).unsqueeze(3).to_broadcast([P, 16, 2, 16]),
-            )
-            nc.vector.transpose(wgt_sb[:], spread[:])
+        def over_plane(a, i, columns, dtype):
+            return keep.tile([P, columns], dtype, name=f"x_{a}_{i}", align_bytes=DMA_ALIGN)
 
         def load_w(h):
             rows = w[2 * h * K_PASS : 2 * (h + 1) * K_PASS, :]
             nc.sync.dma_start(w_pairs[h][:], rows.rearrange("(a p i) n -> p a i n", a=2, i=PACK))
 
-        def load_planes(a, i, count):
-            tile = keep.tile([P, count * T], F32, name=f"x_{a}_{i}", align_bytes=256)
+        def load_wgt():
+            rows = keep.tile([P, 32], F32, name="wgt_rows", align_bytes=DMA_ALIGN)
+            turned = keep.tile([P, 32], F32, name="wgt_turned", align_bytes=MX_ALIGN)
+            spread = keep.tile([P, S], F32, name="wgt_spread", align_bytes=MX_ALIGN)
+            half_rows = wgt.rearrange("p (h c) -> (p h) c", h=2)
+            nc.sync.dma_start(rows[:], half_rows[0 : 2 * P : 17, :].rearrange("u (b c) -> u b c", c=32))
+            nc.vector.transpose(turned[:], rows[:])
+            nc.scalar.copy(
+                spread[:].rearrange("p (b g s) -> p b g s", g=2, s=LIST_ROWS),
+                turned[:].rearrange("p (g b) -> p b g", g=2).unsqueeze(3).to_broadcast([P, 16, 2, LIST_ROWS]),
+            )
+            nc.vector.transpose(wgt_sb[:], spread[:])
+
+        def load_plane(a, i):
             rows = xT[a * K_PASS : (a + 1) * K_PASS, :].rearrange("(p i) t -> p (i t)", i=PACK)
-            nc.sync.dma_start(tile[:], rows[:, i * T : (i + count) * T])
-            planes.setdefault((a, i), tile)
+            plane = over_plane(a, i, T, F32)
+            nc.sync.dma_start(plane[:], rows[:, i * T : (i + 1) * T])
+            planes.setdefault((a, i), plane)
 
         load_w(0)
         nc.sync.dma_start(offs_sb[:], offs)
         load_wgt()
-        load_planes(0, 0, 2 if (0, 0) in PAIRS else 1)
+        load_plane(0, 0)
         load_w(1)
         for a in range(PASSES):
             for i in range(PACK):
-                if (a, i) != (0, 0) and (a, i - 1) not in PAIRS:
-                    load_planes(a, i, 2 if (a, i) in PAIRS else 1)
+                if (a, i) != (0, 0):
+                    load_plane(a, i)
 
-        x_codes = {a: keep.tile([P, S], U32, name=f"xc_{a}", align_bytes=64) for a in (0, 1, 3)}
-        x_scales = [keep.tile([P, S], U8, name=f"xs_{a}", align_bytes=64) for a in range(PASSES)]
-        w_codes = [keep.tile([P, 2 * M], U32, name=f"wc_{a}", align_bytes=64) for a in range(PASSES)]
-        w_scales = [keep.tile([P, 2 * M], U8, name=f"ws_{a}", align_bytes=64) for a in range(PASSES)]
-        sums = [[(slice(0, M), psum.tile([J_TILE, M], F32, name=f"sum_{j}"))] for j in range(3)]
-        sums.append([(slice(h, h + 128), psum.tile([J_TILE, 128], F32, name=f"sum_3_{h}")) for h in (0, 128)])
+        whole_codes = {a: over_plane(a + 1, PACK - 1, S, U32) for a in (0, 1)}
+        whole_codes.setdefault(LAST, keep.tile([P, S], U32, name="last_codes", align_bytes=MX_ALIGN))
+        x_codes = {(a, j): whole_codes[a][:, j * J_TILE : (j + 1) * J_TILE] for a in whole_codes for j in range(TILES)}
+        x_scales = [keep.tile([P, S], U8, name=f"xs_{a}", align_bytes=MX_ALIGN) for a in range(PASSES)]
+        w_codes = [keep.tile([P, 2 * M], U32, name=f"wc_{a}", align_bytes=MX_ALIGN) for a in range(PASSES)]
+        w_scales = [keep.tile([P, 2 * M], U8, name=f"ws_{a}", align_bytes=MX_ALIGN) for a in range(PASSES)]
+        sums = [[(slice(0, M), psum.tile([J_TILE, M], F32, name=f"sum_{j}"))] for j in range(TILES - 1)]
+        sums.append(
+            [(slice(n, n + M // 2), psum.tile([J_TILE, M // 2], F32, name=f"sum_last_{n}")) for n in (0, M // 2)]
+        )
 
-        def round_to(columns, planes_f32):
+        def round_four_planes(columns, values):
             nc.scalar.copy(
-                columns.rearrange("p (c m) i -> p c i m", m=4), planes_f32.rearrange("p i (c m) -> p c i m", m=4)
+                columns.rearrange("p (c m) i -> p c i m", m=4), values.rearrange("p i (c m) -> p c i m", m=4)
             )
 
         def split_w(a):
-            hi = work.tile([P, PACK, M], F32, name="w_hi", align_bytes=256)
+            hi = work.tile([P, PACK, M], F32, name="w_hi")
             lo = work.tile([P, PACK, M], F32, name="w_lo")
-            rounded = work.tile([P, 2 * M, PACK], BF16, name="w_rounded", align_bytes=64)
+            rounded = work.tile([P, 2 * M, PACK], BF16, name="w_rounded", align_bytes=MX_ALIGN)
             nc.vector.tensor_scalar(hi[:].bitcast(I32), w_f32[a].bitcast(I32), HI_MASK, None, AND)
             nc.vector.tensor_tensor(lo[:], w_f32[a], hi[:], SUB)
-            round_to(rounded[:, :M, :], hi[:])
-            round_to(rounded[:, M:, :], lo[:])
+            round_four_planes(rounded[:, :M, :], hi[:])
+            round_four_planes(rounded[:, M:, :], lo[:])
             return rounded
 
         def quantise_w(a, rounded):
@@ -101,140 +114,104 @@ def tile_list_heads_tm_hl_none_kernel(tc, xT, w, wgt, offs, out):
 
         def pick(a, i, j0, width, picked):
             nc.vector.tensor_tensor(
-                picked,
-                planes[a, i][:].indirect(offs_sb[:, j0 // 16 : (j0 + width) // 16]),
+                picked[:, i, j0 : j0 + width],
+                planes[a, i][:].indirect(offs_sb[:, j0 // LIST_ROWS : (j0 + width) // LIST_ROWS]),
                 wgt_sb[:, j0 : j0 + width],
                 MULT,
             )
 
-        def codes_of(a, j0, width):
-            if a == 2:
-                return late_codes[j0 // 256][:, j0 % 256 : j0 % 256 + width]
-            return x_codes[a][:, j0 : j0 + width]
-
-        late_codes = []
-
-        def quantise(a, j0, width, rounded):
+        def quantise_x(a, j0, codes, rounded):
+            width = rounded.shape[1]
             nc.vector.quantize_mx(
-                out=codes_of(a, j0, width).bitcast(FP8X4), scales=x_scales[a][:, j0 : j0 + width], in_=rounded
+                out=codes.bitcast(FP8X4),
+                scales=x_scales[a][:, j0 : j0 + width],
+                in_=rounded.rearrange("p j i -> p (j i)"),
             )
 
         def multiply(a, j):
-            cols = slice(j * J_TILE, (j + 1) * J_TILE)
             for n_cols, total in sums[j]:
                 for part in range(2):
                     w_cols = slice(part * M + n_cols.start, part * M + n_cols.stop)
                     nc.tensor.matmul_mx(
                         out=total[:],
-                        lhsT=codes_of(a, cols.start, J_TILE).bitcast(FP8X4),
-                        lhsT_scale=x_scales[a][:, cols],
+                        lhsT=x_codes[a, j].bitcast(FP8X4),
+                        lhsT_scale=x_scales[a][:, j * J_TILE : (j + 1) * J_TILE],
                         rhs=w_codes[a][:, w_cols].bitcast(FP8X4),
                         rhs_scale=w_scales[a][:, w_cols],
                         start=(a == 0 and part == 0),
-                        stop=(a == PASSES - 1 and part == 1),
+                        stop=(a == LAST and part == 1),
                     )
 
-        def finish(a, rounded):
-            quantise(a, 0, S, rounded[:].rearrange("p j i -> p (j i)"))
-            for j in range(S // J_TILE):
-                multiply(a, j)
-
-        w_rounded = [split_w(0), split_w(1)]
-        waiting = []
-        picked_before = None
-
-        def round_pass(a, values):
-            rounded = keep.tile([P, S, PACK], BF16, name=f"rounded_{a % 2}", align_bytes=64)
+        def round_pass(a, picked):
+            rounded = keep.tile([P, S, PACK], BF16, name=f"rounded_{a % 2}", align_bytes=MX_ALIGN)
             for j0 in range(0, S, J_TILE):
-                round_to(rounded[:, j0 : j0 + J_TILE, :], values[:, :, j0 : j0 + J_TILE])
-            waiting.append(rounded)
+                round_four_planes(rounded[:, j0 : j0 + J_TILE, :], picked[:, :, j0 : j0 + J_TILE])
+            return rounded
 
-        for a in range(PASSES - 1):
+        def pick_pass(a):
             picked = work.tile([P, PACK, S], F32, name="picked")
             for i in range(PACK):
-                if (a, i) in PAIRS:
-                    second = work.tile([P, T], F32, name="second")
-                    nc.scalar.copy(second[:], planes[a, i][:, T:])
-                    planes.setdefault((a, i + 1), second)
-                    for j0 in (0, 256):
-                        pick(a, i, j0, 256, picked[:, i, j0 : j0 + 256])
-                else:
-                    pick(a, i, 0, S, picked[:, i, :])
-                if a == 0 and i == 0:
-                    for b in range(2):
+                pick(a, i, 0, S, picked)
+                if a == 0 and i < 2:
+                    for b in (2 * i, 2 * i + 1):
                         quantise_w(b, w_rounded[b])
-                    w_rounded = [split_w(2), split_w(3)]
-                if a == 0 and i == 1:
-                    for b in range(2):
-                        quantise_w(b + 2, w_rounded[b])
-                if a > 0 and i == 2:
-                    round_pass(a - 1, picked_before)
-                if a == 2 and i == 0:
-                    finish(0, waiting[0])
-                if a == 2 and i == 3:
-                    quantise(1, 0, S, waiting[1][:].rearrange("p j i -> p (j i)"))
-            picked_before = picked
-        round_pass(PASSES - 2, picked_before)
+                if a == 0 and i == 0:
+                    w_rounded.extend([split_w(2), split_w(3)])
+            return round_pass(a, picked)
 
-        a = PASSES - 1
-        tiles = S // J_TILE
-        vector_tile = 3
-        rounded_last = [keep.tile([P, J_TILE, PACK], BF16, name=f"rounded_last_{j}", align_bytes=64) for j in range(tiles)]
+        w_rounded = [split_w(0), split_w(1)]
+        x_rounded = []
+        for a in range(LAST):
+            x_rounded.append(pick_pass(a))
+            if a > 0:
+                quantise_x(a - 1, 0, whole_codes[a - 1][:], x_rounded[a - 1][:])
+            if a == 1:
+                for j in range(TILES):
+                    multiply(0, j)
+
         picked = work.tile([P, PACK, S], F32, name="picked")
+        last_rounded = [
+            keep.tile([P, J_TILE, PACK], BF16, name=f"last_rounded_{j}", align_bytes=MX_ALIGN) for j in range(TILES)
+        ]
 
-        def round_last(j, i0, i1):
-            source = picked[:, i0:i1, j * J_TILE : (j + 1) * J_TILE].rearrange("p i j -> p j i")
-            if j == vector_tile:
-                nc.vector.tensor_copy(rounded_last[j][:, :, i0:i1], source)
-            else:
-                nc.scalar.copy(rounded_last[j][:, :, i0:i1], source)
+        def round_last(engine_copy, j, i0, i1, c0, c1):
+            values = picked[:, i0:i1, j * J_TILE + c0 : j * J_TILE + c1]
+            engine_copy(last_rounded[j][:, c0:c1, i0:i1], values.rearrange("p i j -> p j i"))
 
-        for i in range(PACK - 1):
-            for j0 in (0, 256):
-                pick(a, i, j0, 256, picked[:, i, j0 : j0 + 256])
+        pick(LAST, 0, 0, S, picked)
+        for i in (1, 2):
+            for j0 in (0, HALF):
+                pick(LAST, i, j0, HALF, picked)
                 for j in (j0 // J_TILE, j0 // J_TILE + 1):
-                    if j != vector_tile and i > 0:
-                        round_last(j, 0 if i == 1 else i, i + 1)
-            if i > 0:
-                late_codes.append(keep.tile([P, 256], U32, name=f"x_3_{i}", align_bytes=256))
-                j0 = (i - 1) * 256
-                quantise(2, j0, 256, waiting[2][:, j0 : j0 + 256, :].rearrange("p j i -> p (j i)"))
-                for j in (j0 // J_TILE, j0 // J_TILE + 1):
-                    multiply(2, j)
-                    multiply(1, j)
-            if i == 1:
-                round_last(vector_tile, 0, 2)
+                    if i == 1:
+                        round_last(nc.scalar.copy, j, 0, 2, 0, J_TILE)
+                    else:
+                        round_last(nc.scalar.copy, j, 2, 3, 0, SCALAR_COLUMNS[j])
+            j0 = (i - 1) * HALF
+            codes = over_plane(LAST, i, HALF, U32)
+            quantise_x(2, j0, codes[:], x_rounded[2][:, j0 : j0 + HALF, :])
+            for c0 in (0, J_TILE):
+                j = (j0 + c0) // J_TILE
+                x_codes.setdefault((2, j), codes[:, c0 : c0 + J_TILE])
+                multiply(2, j)
+                multiply(1, j)
 
-        results = work.tile([J_TILE, tiles, M], F32, name="w_hi", align_bytes=256)
+        for j in range(TILES):
+            pick(LAST, PACK - 1, j * J_TILE, J_TILE, picked)
+            round_last(nc.scalar.copy, j, PACK - 1, PACK, 0, SCALAR_COLUMNS[j])
+        for j in range(TILES):
+            quantise_x(LAST, j * J_TILE, x_codes[LAST, j], last_rounded[j][:])
+            multiply(LAST, j)
+            if j == 0:
+                for shared in range(TILES):
+                    if SCALAR_COLUMNS[shared] < J_TILE:
+                        round_last(nc.vector.tensor_copy, shared, 2, PACK, SCALAR_COLUMNS[shared], J_TILE)
 
-        def pick_last(j):
-            j0 = j * J_TILE
-            pick(a, PACK - 1, j0, J_TILE, picked[:, PACK - 1, j0 : j0 + J_TILE])
-            if j != vector_tile:
-                round_last(j, PACK - 1, PACK)
-
-        def finish_last(j):
-            quantise(a, j * J_TILE, J_TILE, rounded_last[j][:].rearrange("p j i -> p (j i)"))
-            multiply(a, j)
-
-        def store(j):
+        results = keep.tile([J_TILE, TILES, M], F32, name="results", align_bytes=DMA_ALIGN)
+        for j in range(TILES):
             for n_cols, total in sums[j]:
-                if j == 2 or (j == 3 and n_cols.start > 0):
+                if j == TILES - 2 or n_cols.start > 0:
                     nc.vector.tensor_copy(results[:, j, n_cols], total[:])
                 else:
                     nc.scalar.copy(results[:, j, n_cols], total[:])
             nc.sync.dma_start(out[j * J_TILE : (j + 1) * J_TILE, :], results[:, j, :])
-
-        pick_last(0)
-        pick_last(1)
-        pick_last(2)
-        pick_last(3)
-        finish_last(0)
-        round_last(vector_tile, 2, PACK)
-        finish_last(1)
-        finish_last(2)
-        finish_last(3)
-        store(0)
-        store(1)
-        store(2)
-        store(3)

@@ -25,10 +25,12 @@ J_TILE = 128
 TILES = S // J_TILE
 HALF = S // 2
 LIST_ROWS = 16
-HI_MASK = -0x00100000
+HI_PAIR_MASK = -0x000F0010
 MX_ALIGN = 64
 DMA_ALIGN = 256
 SCALAR_COLUMNS = (128, 128, 96, 64)
+VECTOR_MOVE = 768
+PAIRS = 4
 
 
 def tile_list_heads_tm_hl_none_kernel(tc, xT, w, wgt, offs, out):
@@ -40,17 +42,8 @@ def tile_list_heads_tm_hl_none_kernel(tc, xT, w, wgt, offs, out):
         psum = ctx.enter_context(tc.psum_pool(name="psum", bufs=1))
 
         offs_sb = lists.tile([P, S // LIST_ROWS], U16, name="offs_sb", align_bytes=DMA_ALIGN)
-        w_pairs = [keep.tile([P, 2, PACK, M], F32, name=f"w_{h}", align_bytes=DMA_ALIGN) for h in range(PASSES // 2)]
-        w_f32 = [w_pairs[a // 2][:, a % 2] for a in range(PASSES)]
+        w_sb = [keep.tile([P, PACK, M], F32, name=f"w_{a}", align_bytes=DMA_ALIGN)[:] for a in range(PASSES)]
         wgt_sb = keep.tile([P, S], F32, name="wgt_sb", align_bytes=MX_ALIGN)
-        planes = {}
-
-        def over_plane(a, i, columns, dtype):
-            return keep.tile([P, columns], dtype, name=f"x_{a}_{i}", align_bytes=DMA_ALIGN)
-
-        def load_w(h):
-            rows = w[2 * h * K_PASS : 2 * (h + 1) * K_PASS, :]
-            nc.sync.dma_start(w_pairs[h][:], rows.rearrange("(a p i) n -> p a i n", a=2, i=PACK))
 
         def load_wgt():
             rows = keep.tile([P, 32], F32, name="wgt_rows", align_bytes=DMA_ALIGN)
@@ -65,67 +58,64 @@ def tile_list_heads_tm_hl_none_kernel(tc, xT, w, wgt, offs, out):
             )
             nc.vector.transpose(wgt_sb[:], spread[:])
 
-        def load_plane(a, i):
+        def x_tile(a, i, columns, dtype):
+            return keep.tile([P, columns], dtype, name=f"x_{a}_{i}", align_bytes=DMA_ALIGN)
+
+        def load_planes(a, i, count):
             rows = xT[a * K_PASS : (a + 1) * K_PASS, :].rearrange("(p i) t -> p (i t)", i=PACK)
-            plane = over_plane(a, i, T, F32)
-            nc.sync.dma_start(plane[:], rows[:, i * T : (i + 1) * T])
-            planes.setdefault((a, i), plane)
+            tile = x_tile(a, i, count * T, F32)
+            nc.sync.dma_start(tile[:], rows[:, i * T : (i + count) * T])
+            return tile
 
-        load_w(0)
-        nc.sync.dma_start(offs_sb[:], offs)
+        w_rows = w.rearrange("(a p i) n -> a p i n", a=PASSES, i=PACK)
+        nc.sync.dma_start(w_sb[0], w_rows[0])
         load_wgt()
-        load_plane(0, 0)
-        load_w(1)
-        for a in range(PASSES):
-            for i in range(PACK):
-                if (a, i) != (0, 0):
-                    load_plane(a, i)
+        nc.sync.dma_start(offs_sb[:], offs)
+        for a in range(1, PASSES):
+            nc.sync.dma_start(w_sb[a], w_rows[a])
+        loaded = {(n // PACK, n % PACK): load_planes(n // PACK, n % PACK, 2) for n in range(0, 2 * PAIRS, 2)}
+        for n in range(2 * PAIRS, PASSES * PACK):
+            loaded.setdefault((n // PACK, n % PACK), load_planes(n // PACK, n % PACK, 1))
 
-        whole_codes = {a: over_plane(a + 1, PACK - 1, S, U32) for a in (0, 1)}
-        whole_codes.setdefault(LAST, keep.tile([P, S], U32, name="last_codes", align_bytes=MX_ALIGN))
-        x_codes = {(a, j): whole_codes[a][:, j * J_TILE : (j + 1) * J_TILE] for a in whole_codes for j in range(TILES)}
         x_scales = [keep.tile([P, S], U8, name=f"xs_{a}", align_bytes=MX_ALIGN) for a in range(PASSES)]
         w_codes = [keep.tile([P, 2 * M], U32, name=f"wc_{a}", align_bytes=MX_ALIGN) for a in range(PASSES)]
         w_scales = [keep.tile([P, 2 * M], U8, name=f"ws_{a}", align_bytes=MX_ALIGN) for a in range(PASSES)]
+        whole_codes = {a: keep.tile([P, S], U32, name=f"xc_{a}", align_bytes=MX_ALIGN) for a in (0, 1, LAST)}
+        x_codes = {(a, j): whole_codes[a][:, j * J_TILE : (j + 1) * J_TILE] for a in whole_codes for j in range(TILES)}
         sums = [[(slice(0, M), psum.tile([J_TILE, M], F32, name=f"sum_{j}"))] for j in range(TILES - 1)]
         sums.append(
             [(slice(n, n + M // 2), psum.tile([J_TILE, M // 2], F32, name=f"sum_last_{n}")) for n in (0, M // 2)]
         )
 
-        def round_four_planes(columns, values):
-            nc.scalar.copy(
-                columns.rearrange("p (c m) i -> p c i m", m=4), values.rearrange("p i (c m) -> p c i m", m=4)
-            )
+        def by_lines(columns):
+            return columns.rearrange("p (c m) i -> p c i m", m=4)
 
-        def split_w(a):
-            hi = work.tile([P, PACK, M], F32, name="w_hi")
-            lo = work.tile([P, PACK, M], F32, name="w_lo")
-            rounded = work.tile([P, 2 * M, PACK], BF16, name="w_rounded", align_bytes=MX_ALIGN)
-            nc.vector.tensor_scalar(hi[:].bitcast(I32), w_f32[a].bitcast(I32), HI_MASK, None, AND)
-            nc.vector.tensor_tensor(lo[:], w_f32[a], hi[:], SUB)
-            round_four_planes(rounded[:, :M, :], hi[:])
-            round_four_planes(rounded[:, M:, :], lo[:])
-            return rounded
+        def by_planes(values):
+            return values.rearrange("p i (c m) -> p c i m", m=4)
 
-        def quantise_w(a, rounded):
-            nc.vector.quantize_mx(
-                out=w_codes[a][:].bitcast(FP8X4), scales=w_scales[a][:], in_=rounded[:].rearrange("p n i -> p (n i)")
-            )
+        def rounded_tile(a):
+            return keep.tile([P, 2 * M, PACK], BF16, name=f"rounded_{a}", align_bytes=MX_ALIGN)
 
-        def pick(a, i, j0, width, picked):
+        def quantise(codes, scales, rounded):
+            nc.vector.quantize_mx(out=codes.bitcast(FP8X4), scales=scales, in_=rounded.rearrange("p j i -> p (j i)"))
+
+        w_rounded = [rounded_tile(a) for a in range(PASSES)]
+        for a in range(PASSES):
+            hi = w_rounded[a][:, :M, :]
+            nc.scalar.copy(by_lines(hi), by_planes(w_sb[a].bitcast(BF16)[:, :, 1::2]))
+            pairs = hi.rearrange("p n i -> p (n i)").bitcast(I32)
+            nc.vector.tensor_scalar(pairs, pairs, HI_PAIR_MASK, None, AND)
+            if a > 0:
+                quantise(w_codes[a - 1][:], w_scales[a - 1][:], w_rounded[a - 1][:])
+            nc.vector.tensor_tensor(by_lines(w_rounded[a][:, M:, :]), by_planes(w_sb[a]), by_lines(hi), SUB)
+        quantise(w_codes[LAST][:], w_scales[LAST][:], w_rounded[LAST][:])
+
+        def pick(window, i, j0, width, picked):
             nc.vector.tensor_tensor(
                 picked[:, i, j0 : j0 + width],
-                planes[a, i][:].indirect(offs_sb[:, j0 // LIST_ROWS : (j0 + width) // LIST_ROWS]),
+                window[:].indirect(offs_sb[:, j0 // LIST_ROWS : (j0 + width) // LIST_ROWS]),
                 wgt_sb[:, j0 : j0 + width],
                 MULT,
-            )
-
-        def quantise_x(a, j0, codes, rounded):
-            width = rounded.shape[1]
-            nc.vector.quantize_mx(
-                out=codes.bitcast(FP8X4),
-                scales=x_scales[a][:, j0 : j0 + width],
-                in_=rounded.rearrange("p j i -> p (j i)"),
             )
 
         def multiply(a, j):
@@ -142,70 +132,80 @@ def tile_list_heads_tm_hl_none_kernel(tc, xT, w, wgt, offs, out):
                         stop=(a == LAST and part == 1),
                     )
 
-        def round_pass(a, picked):
-            rounded = keep.tile([P, S, PACK], BF16, name=f"rounded_{a % 2}", align_bytes=MX_ALIGN)
-            for j0 in range(0, S, J_TILE):
-                round_four_planes(rounded[:, j0 : j0 + J_TILE, :], picked[:, :, j0 : j0 + J_TILE])
-            return rounded
+        def round_half(rounded, values):
+            for j0 in range(0, HALF, J_TILE):
+                nc.scalar.copy(by_lines(rounded[:, j0 : j0 + J_TILE, :]), by_planes(values[:, :, j0 : j0 + J_TILE]))
 
-        def pick_pass(a):
-            picked = work.tile([P, PACK, S], F32, name="picked")
-            for i in range(PACK):
-                pick(a, i, 0, S, picked)
-                if a == 0 and i < 2:
-                    for b in (2 * i, 2 * i + 1):
-                        quantise_w(b, w_rounded[b])
-                if a == 0 and i == 0:
-                    w_rounded.extend([split_w(2), split_w(3)])
-            return round_pass(a, picked)
-
-        w_rounded = [split_w(0), split_w(1)]
-        x_rounded = []
+        picks = []
         for a in range(LAST):
-            x_rounded.append(pick_pass(a))
-            if a > 0:
-                quantise_x(a - 1, 0, whole_codes[a - 1][:], x_rounded[a - 1][:])
+            picked = work.tile([P, PACK, S], F32, name="picked")
+            picks.append(picked)
+            for i in (0, 2):
+                if (a, i + 1) in loaded:
+                    pick(loaded[a, i], i, 0, S, picked)
+                    second = loaded[a, i + 1]
+                else:
+                    second = work.tile([P, T], F32, name="second", align_bytes=DMA_ALIGN)
+                    for j0 in (0, HALF):
+                        pick(loaded[a, i], i, j0, HALF, picked)
+                    split = VECTOR_MOVE if a > 0 else 0
+                    if split > 0:
+                        nc.vector.tensor_copy(second[:, :split], loaded[a, i][:, T : T + split])
+                    nc.scalar.copy(second[:, split:], loaded[a, i][:, T + split :])
+                pick(second, i + 1, 0, S, picked)
+                if a > 0 and i == 0:
+                    rounded = x_tile(a, 0, S * PACK, BF16)[:].rearrange("p (j i) -> p j i", i=PACK)
+                    for j0 in (0, HALF):
+                        round_half(rounded[:, j0 : j0 + HALF, :], picks[a - 1][:, :, j0 : j0 + HALF])
+                if a > 0:
+                    cols = slice(i // 2 * HALF, i // 2 * HALF + HALF)
+                    quantise(whole_codes[a - 1][:, cols], x_scales[a - 1][:, cols], rounded[:, cols, :])
             if a == 1:
                 for j in range(TILES):
                     multiply(0, j)
+        rounded_2 = rounded_tile(0)
+        for j0 in (0, HALF):
+            round_half(rounded_2[:, j0 : j0 + HALF, :], picks[2][:, :, j0 : j0 + HALF])
 
         picked = work.tile([P, PACK, S], F32, name="picked")
         last_rounded = [
             keep.tile([P, J_TILE, PACK], BF16, name=f"last_rounded_{j}", align_bytes=MX_ALIGN) for j in range(TILES)
         ]
 
-        def round_last(engine_copy, j, i0, i1, c0, c1):
-            values = picked[:, i0:i1, j * J_TILE + c0 : j * J_TILE + c1]
-            engine_copy(last_rounded[j][:, c0:c1, i0:i1], values.rearrange("p i j -> p j i"))
+        def round_last(j, i0, i1, engine_copy, c0, c1):
+            if c0 < c1:
+                values = picked[:, i0:i1, j * J_TILE + c0 : j * J_TILE + c1]
+                engine_copy(by_lines(last_rounded[j][:, c0:c1, i0:i1]), by_planes(values))
 
-        pick(LAST, 0, 0, S, picked)
-        for i in (1, 2):
-            for j0 in (0, HALF):
-                pick(LAST, i, j0, HALF, picked)
-                for j in (j0 // J_TILE, j0 // J_TILE + 1):
-                    if i == 1:
-                        round_last(nc.scalar.copy, j, 0, 2, 0, J_TILE)
-                    else:
-                        round_last(nc.scalar.copy, j, 2, 3, 0, SCALAR_COLUMNS[j])
-            j0 = (i - 1) * HALF
-            codes = over_plane(LAST, i, HALF, U32)
-            quantise_x(2, j0, codes[:], x_rounded[2][:, j0 : j0 + HALF, :])
+        def finish_pass_2(j0, i):
+            codes = x_tile(LAST, i, HALF, U32)
+            quantise(codes[:], x_scales[2][:, j0 : j0 + HALF], rounded_2[:, j0 : j0 + HALF, :])
             for c0 in (0, J_TILE):
                 j = (j0 + c0) // J_TILE
                 x_codes.setdefault((2, j), codes[:, c0 : c0 + J_TILE])
                 multiply(2, j)
                 multiply(1, j)
 
+        pick(loaded[LAST, 0], 0, 0, S, picked)
+        pick(loaded[LAST, 1], 1, 0, S, picked)
+        finish_pass_2(0, 1)
+        for j in (2, 3):
+            round_last(j, 0, 2, nc.scalar.copy, 0, J_TILE)
+        for j0 in (0, HALF):
+            pick(loaded[LAST, 2], 2, j0, HALF, picked)
         for j in range(TILES):
-            pick(LAST, PACK - 1, j * J_TILE, J_TILE, picked)
-            round_last(nc.scalar.copy, j, PACK - 1, PACK, 0, SCALAR_COLUMNS[j])
+            round_last(j, 0 if j < 2 else 2, 3, nc.scalar.copy, 0, SCALAR_COLUMNS[j])
+        finish_pass_2(HALF, 2)
+
         for j in range(TILES):
-            quantise_x(LAST, j * J_TILE, x_codes[LAST, j], last_rounded[j][:])
+            pick(loaded[LAST, PACK - 1], PACK - 1, j * J_TILE, J_TILE, picked)
+            round_last(j, PACK - 1, PACK, nc.scalar.copy, 0, SCALAR_COLUMNS[j])
+        for j in range(TILES):
+            quantise(x_codes[LAST, j], x_scales[LAST][:, j * J_TILE : (j + 1) * J_TILE], last_rounded[j][:])
             multiply(LAST, j)
             if j == 0:
                 for shared in range(TILES):
-                    if SCALAR_COLUMNS[shared] < J_TILE:
-                        round_last(nc.vector.tensor_copy, shared, 2, PACK, SCALAR_COLUMNS[shared], J_TILE)
+                    round_last(shared, 2, PACK, nc.vector.tensor_copy, SCALAR_COLUMNS[shared], J_TILE)
 
         results = keep.tile([J_TILE, TILES, M], F32, name="results", align_bytes=DMA_ALIGN)
         for j in range(TILES):
@@ -214,4 +214,4 @@ def tile_list_heads_tm_hl_none_kernel(tc, xT, w, wgt, offs, out):
                     nc.vector.tensor_copy(results[:, j, n_cols], total[:])
                 else:
                     nc.scalar.copy(results[:, j, n_cols], total[:])
-            nc.sync.dma_start(out[j * J_TILE : (j + 1) * J_TILE, :], results[:, j, :])
+                nc.sync.dma_start(out[j * J_TILE : (j + 1) * J_TILE, n_cols], results[:, j, n_cols])

@@ -50,7 +50,7 @@ def tile_list_heads_tm_hl_none_kernel(tc, xT, w, wgt, offs, out):
             turned = keep.tile([P, 32], F32, name="wgt_turned", align_bytes=MX_ALIGN)
             spread = keep.tile([P, S], F32, name="wgt_spread", align_bytes=MX_ALIGN)
             half_rows = wgt.rearrange("p (h c) -> (p h) c", h=2)
-            nc.sync.dma_start(rows[:], half_rows[0 : 2 * P : 17, :].rearrange("u (b c) -> u b c", c=32))
+            nc.scalar.dma_start(rows[:], half_rows[0 : 2 * P : 17, :].rearrange("u (b c) -> u b c", c=32))
             nc.vector.transpose(turned[:], rows[:])
             nc.scalar.copy(
                 spread[:].rearrange("p (b g s) -> p b g s", g=2, s=LIST_ROWS),
@@ -214,4 +214,5 @@ def tile_list_heads_tm_hl_none_kernel(tc, xT, w, wgt, offs, out):
                     nc.vector.tensor_copy(results[:, j, n_cols], total[:])
                 else:
                     nc.scalar.copy(results[:, j, n_cols], total[:])
-                nc.sync.dma_start(out[j * J_TILE : (j + 1) * J_TILE, n_cols], results[:, j, n_cols])
+                queue = nc.scalar if n_cols.start > 0 else nc.sync
+                queue.dma_start(out[j * J_TILE : (j + 1) * J_TILE, n_cols], results[:, j, n_cols])

@@ -80,7 +80,7 @@ def tile_list_heads_tm_hl_none_kernel(tc, xT, w, wgt, offs, out):
         x_scales = [keep.tile([P, S], U8, name=f"xs_{a}", align_bytes=MX_ALIGN) for a in range(PASSES)]
         w_codes = [keep.tile([P, 2 * M], U32, name=f"wc_{a}", align_bytes=MX_ALIGN) for a in range(PASSES)]
         w_scales = [keep.tile([P, 2 * M], U8, name=f"ws_{a}", align_bytes=MX_ALIGN) for a in range(PASSES)]
-        whole_codes = {a: keep.tile([P, S], U32, name=f"xc_{a}", align_bytes=MX_ALIGN) for a in (0, 1, LAST)}
+        whole_codes = {a: keep.tile([P, S], U32, name=f"xc_{a}", align_bytes=MX_ALIGN) for a in (0, LAST)}
         x_codes = {(a, j): whole_codes[a][:, j * J_TILE : (j + 1) * J_TILE] for a in whole_codes for j in range(TILES)}
         sums = [[(slice(0, M), psum.tile([J_TILE, M], F32, name=f"sum_{j}"))] for j in range(TILES - 1)]
         sums.append(
@@ -128,7 +128,7 @@ def tile_list_heads_tm_hl_none_kernel(tc, xT, w, wgt, offs, out):
                         lhsT_scale=x_scales[a][:, j * J_TILE : (j + 1) * J_TILE],
                         rhs=w_codes[a][:, w_cols].bitcast(FP8X4),
                         rhs_scale=w_scales[a][:, w_cols],
-                        start=(a == 0 and part == 0),
+                        start=(a == 1 and part == 0),
                         stop=(a == LAST and part == 1),
                     )
 
@@ -157,12 +157,10 @@ def tile_list_heads_tm_hl_none_kernel(tc, xT, w, wgt, offs, out):
                     rounded = x_tile(a, 0, S * PACK, BF16)[:].rearrange("p (j i) -> p j i", i=PACK)
                     for j0 in (0, HALF):
                         round_half(rounded[:, j0 : j0 + HALF, :], picks[a - 1][:, :, j0 : j0 + HALF])
-                if a > 0:
+                if a == 1:
                     cols = slice(i // 2 * HALF, i // 2 * HALF + HALF)
                     quantise(whole_codes[a - 1][:, cols], x_scales[a - 1][:, cols], rounded[:, cols, :])
-            if a == 1:
-                for j in range(TILES):
-                    multiply(0, j)
+        rounded_1 = rounded
         rounded_2 = rounded_tile(0)
         for j0 in (0, HALF):
             round_half(rounded_2[:, j0 : j0 + HALF, :], picks[2][:, :, j0 : j0 + HALF])
@@ -184,9 +182,14 @@ def tile_list_heads_tm_hl_none_kernel(tc, xT, w, wgt, offs, out):
                 j = (j0 + c0) // J_TILE
                 x_codes.setdefault((2, j), codes[:, c0 : c0 + J_TILE])
                 multiply(2, j)
-                multiply(1, j)
+                multiply(0, j)
 
         pick(loaded[LAST, 0], 0, 0, S, picked)
+        codes_1 = x_tile(LAST, 0, S, U32)
+        quantise(codes_1[:], x_scales[1][:], rounded_1)
+        for j in range(TILES):
+            x_codes.setdefault((1, j), codes_1[:, j * J_TILE : (j + 1) * J_TILE])
+            multiply(1, j)
         pick(loaded[LAST, 1], 1, 0, S, picked)
         finish_pass_2(0, 1)
         for j in (2, 3):

@@ -26,7 +26,7 @@ TILES = S // J_TILE
 HALF = S // 2
 LIST_ROWS = 16
 HI_PAIR_MASK = -0x000F0010
-MX_ALIGN = 64
+MX_ALIGN = 256
 DMA_ALIGN = 256
 SCALAR_COLUMNS = (128, 128, 96, 64)
 VECTOR_MOVE = 768

from contextlib import ExitStack

import concourse.mybir as mybir

K, M, T, S = 2048, 256, 2048, 512
FLOPS = 2 * 2 * K * M * S

F32 = mybir.dt.float32
BF16 = mybir.dt.bfloat16
I32 = mybir.dt.int32
U32 = mybir.dt.uint32
U16 = mybir.dt.uint16
U8 = mybir.dt.uint8
FP8X4 = mybir.dt.float8_e4m3fn_x4
MULT = mybir.AluOpType.mult
SUB = mybir.AluOpType.subtract
AND = mybir.AluOpType.bitwise_and

P = 128
PACK = 4
K_PASS = P * PACK
PASSES = K // K_PASS
LAST = PASSES - 1
J_TILE = 128
TILES = S // J_TILE
HALF = S // 2
LIST_ROWS = 16
HI_PAIR_MASK = -0x000F0010
MX_ALIGN = 256
DMA_ALIGN = 256
SCALAR_COLUMNS = (128, 128, 96, 64)
VECTOR_MOVE = 768
PAIRS = 4


def tile_list_heads_tm_hl_none_kernel(tc, xT, w, wgt, offs, out):
    nc = tc.nc
    with ExitStack() as ctx:
        lists = ctx.enter_context(tc.tile_pool(name="lists", bufs=1))
        keep = ctx.enter_context(tc.tile_pool(name="keep", bufs=1))
        work = ctx.enter_context(tc.tile_pool(name="work", bufs=2))
        psum = ctx.enter_context(tc.psum_pool(name="psum", bufs=1))

        offs_sb = lists.tile([P, S // LIST_ROWS], U16, name="offs_sb", align_bytes=DMA_ALIGN)
        w_sb = [keep.tile([P, PACK, M], F32, name=f"w_{a}", align_bytes=DMA_ALIGN)[:] for a in range(PASSES)]
        wgt_sb = keep.tile([P, S], F32, name="wgt_sb", align_bytes=MX_ALIGN)

        def load_wgt():
            rows = keep.tile([P, 32], F32, name="wgt_rows", align_bytes=DMA_ALIGN)
            turned = keep.tile([P, 32], F32, name="wgt_turned", align_bytes=MX_ALIGN)
            spread = keep.tile([P, S], F32, name="wgt_spread", align_bytes=MX_ALIGN)
            half_rows = wgt.rearrange("p (h c) -> (p h) c", h=2)
            nc.scalar.dma_start(rows[:], half_rows[0 : 2 * P : 17, :].rearrange("u (b c) -> u b c", c=32))
            nc.vector.transpose(turned[:], rows[:])
            nc.scalar.copy(
                spread[:].rearrange("p (b g s) -> p b g s", g=2, s=LIST_ROWS),
                turned[:].rearrange("p (g b) -> p b g", g=2).unsqueeze(3).to_broadcast([P, 16, 2, LIST_ROWS]),
            )
            nc.vector.transpose(wgt_sb[:], spread[:])

        def x_tile(a, i, columns, dtype):
            return keep.tile([P, columns], dtype, name=f"x_{a}_{i}", align_bytes=DMA_ALIGN)

        def load_planes(a, i, count):
            rows = xT[a * K_PASS : (a + 1) * K_PASS, :].rearrange("(p i) t -> p (i t)", i=PACK)
            tile = x_tile(a, i, count * T, F32)
            nc.sync.dma_start(tile[:], rows[:, i * T : (i + count) * T])
            return tile

        w_rows = w.rearrange("(a p i) n -> a p i n", a=PASSES, i=PACK)
        nc.sync.dma_start(w_sb[0], w_rows[0])
        load_wgt()
        nc.sync.dma_start(offs_sb[:], offs)
        for a in range(1, PASSES):
            nc.sync.dma_start(w_sb[a], w_rows[a])
        loaded = {(n // PACK, n % PACK): load_planes(n // PACK, n % PACK, 2) for n in range(0, 2 * PAIRS, 2)}
        for n in range(2 * PAIRS, PASSES * PACK):
            loaded.setdefault((n // PACK, n % PACK), load_planes(n // PACK, n % PACK, 1))

        x_scales = [keep.tile([P, S], U8, name=f"xs_{a}", align_bytes=MX_ALIGN) for a in range(PASSES)]
        w_codes = [keep.tile([P, 2 * M], U32, name=f"wc_{a}", align_bytes=MX_ALIGN) for a in range(PASSES)]
        w_scales = [keep.tile([P, 2 * M], U8, name=f"ws_{a}", align_bytes=MX_ALIGN) for a in range(PASSES)]
        whole_codes = {a: keep.tile([P, S], U32, name=f"xc_{a}", align_bytes=MX_ALIGN) for a in (0, LAST)}
        x_codes = {(a, j): whole_codes[a][:, j * J_TILE : (j + 1) * J_TILE] for a in whole_codes for j in range(TILES)}
        sums = [[(slice(0, M), psum.tile([J_TILE, M], F32, name=f"sum_{j}"))] for j in range(TILES - 1)]
        sums.append(
            [(slice(n, n + M // 2), psum.tile([J_TILE, M // 2], F32, name=f"sum_last_{n}")) for n in (0, M // 2)]
        )

        def by_lines(columns):
            return columns.rearrange("p (c m) i -> p c i m", m=4)

        def by_planes(values):
            return values.rearrange("p i (c m) -> p c i m", m=4)

        def rounded_tile(a):
            return keep.tile([P, 2 * M, PACK], BF16, name=f"rounded_{a}", align_bytes=MX_ALIGN)

        def quantise(codes, scales, rounded):
            nc.vector.quantize_mx(out=codes.bitcast(FP8X4), scales=scales, in_=rounded.rearrange("p j i -> p (j i)"))

        w_rounded = [rounded_tile(a) for a in range(PASSES)]
        for a in range(PASSES):
            hi = w_rounded[a][:, :M, :]
            nc.scalar.copy(by_lines(hi), by_planes(w_sb[a].bitcast(BF16)[:, :, 1::2]))
            pairs = hi.rearrange("p n i -> p (n i)").bitcast(I32)
            nc.vector.tensor_scalar(pairs, pairs, HI_PAIR_MASK, None, AND)
            if a > 0:
                quantise(w_codes[a - 1][:], w_scales[a - 1][:], w_rounded[a - 1][:])
            nc.vector.tensor_tensor(by_lines(w_rounded[a][:, M:, :]), by_planes(w_sb[a]), by_lines(hi), SUB)
        quantise(w_codes[LAST][:], w_scales[LAST][:], w_rounded[LAST][:])

        def pick(window, i, j0, width, picked):
            nc.vector.tensor_tensor(
                picked[:, i, j0 : j0 + width],
                window[:].indirect(offs_sb[:, j0 // LIST_ROWS : (j0 + width) // LIST_ROWS]),
                wgt_sb[:, j0 : j0 + width],
                MULT,
            )

        def multiply(a, j):
            for n_cols, total in sums[j]:
                for part in range(2):
                    w_cols = slice(part * M + n_cols.start, part * M + n_cols.stop)
                    nc.tensor.matmul_mx(
                        out=total[:],
                        lhsT=x_codes[a, j].bitcast(FP8X4),
                        lhsT_scale=x_scales[a][:, j * J_TILE : (j + 1) * J_TILE],
                        rhs=w_codes[a][:, w_cols].bitcast(FP8X4),
                        rhs_scale=w_scales[a][:, w_cols],
                        start=(a == 1 and part == 0),
                        stop=(a == LAST and part == 1),
                    )

        def round_half(rounded, values):
            for j0 in range(0, HALF, J_TILE):
                nc.scalar.copy(by_lines(rounded[:, j0 : j0 + J_TILE, :]), by_planes(values[:, :, j0 : j0 + J_TILE]))

        picks = []
        for a in range(LAST):
            picked = work.tile([P, PACK, S], F32, name="picked")
            picks.append(picked)
            for i in (0, 2):
                if (a, i + 1) in loaded:
                    pick(loaded[a, i], i, 0, S, picked)
                    second = loaded[a, i + 1]
                else:
                    second = work.tile([P, T], F32, name="second", align_bytes=DMA_ALIGN)
                    for j0 in (0, HALF):
                        pick(loaded[a, i], i, j0, HALF, picked)
                    split = VECTOR_MOVE if a > 0 else 0
                    if split > 0:
                        nc.vector.tensor_copy(second[:, :split], loaded[a, i][:, T : T + split])
                    nc.scalar.copy(second[:, split:], loaded[a, i][:, T + split :])
                pick(second, i + 1, 0, S, picked)
                if a > 0 and i == 0:
                    rounded = x_tile(a, 0, S * PACK, BF16)[:].rearrange("p (j i) -> p j i", i=PACK)
                    for j0 in (0, HALF):
                        round_half(rounded[:, j0 : j0 + HALF, :], picks[a - 1][:, :, j0 : j0 + HALF])
                if a == 1:
                    cols = slice(i // 2 * HALF, i // 2 * HALF + HALF)
                    quantise(whole_codes[a - 1][:, cols], x_scales[a - 1][:, cols], rounded[:, cols, :])
        rounded_1 = rounded
        rounded_2 = rounded_tile(0)
        for j0 in (0, HALF):
            round_half(rounded_2[:, j0 : j0 + HALF, :], picks[2][:, :, j0 : j0 + HALF])

        picked = work.tile([P, PACK, S], F32, name="picked")
        last_rounded = [
            keep.tile([P, J_TILE, PACK], BF16, name=f"last_rounded_{j}", align_bytes=MX_ALIGN) for j in range(TILES)
        ]

        def round_last(j, i0, i1, engine_copy, c0, c1):
            if c0 < c1:
                values = picked[:, i0:i1, j * J_TILE + c0 : j * J_TILE + c1]
                engine_copy(by_lines(last_rounded[j][:, c0:c1, i0:i1]), by_planes(values))

        def finish_pass_2(j0, i):
            codes = x_tile(LAST, i, HALF, U32)
            quantise(codes[:], x_scales[2][:, j0 : j0 + HALF], rounded_2[:, j0 : j0 + HALF, :])
            for c0 in (0, J_TILE):
                j = (j0 + c0) // J_TILE
                x_codes.setdefault((2, j), codes[:, c0 : c0 + J_TILE])
                multiply(2, j)
                multiply(0, j)

        pick(loaded[LAST, 0], 0, 0, S, picked)
        codes_1 = x_tile(LAST, 0, S, U32)
        quantise(codes_1[:], x_scales[1][:], rounded_1)
        for j in range(TILES):
            x_codes.setdefault((1, j), codes_1[:, j * J_TILE : (j + 1) * J_TILE])
            multiply(1, j)
        pick(loaded[LAST, 1], 1, 0, S, picked)
        finish_pass_2(0, 1)
        for j in (2, 3):
            round_last(j, 0, 2, nc.scalar.copy, 0, J_TILE)
        for j0 in (0, HALF):
            pick(loaded[LAST, 2], 2, j0, HALF, picked)
        for j in range(TILES):
            round_last(j, 0 if j < 2 else 2, 3, nc.scalar.copy, 0, SCALAR_COLUMNS[j])
        finish_pass_2(HALF, 2)

        for j in range(TILES):
            pick(loaded[LAST, PACK - 1], PACK - 1, j * J_TILE, J_TILE, picked)
            round_last(j, PACK - 1, PACK, nc.scalar.copy, 0, SCALAR_COLUMNS[j])
        for j in range(TILES):
            quantise(x_codes[LAST, j], x_scales[LAST][:, j * J_TILE : (j + 1) * J_TILE], last_rounded[j][:])
            multiply(LAST, j)
            if j == 0:
                for shared in range(TILES):
                    round_last(shared, 2, PACK, nc.vector.tensor_copy, SCALAR_COLUMNS[shared], J_TILE)

        results = keep.tile([J_TILE, TILES, M], F32, name="results", align_bytes=DMA_ALIGN)
        for j in range(TILES):
            for n_cols, total in sums[j]:
                if j == TILES - 2 or n_cols.start > 0:
                    nc.vector.tensor_copy(results[:, j, n_cols], total[:])
                else:
                    nc.scalar.copy(results[:, j, n_cols], total[:])
                queue = nc.scalar if n_cols.start > 0 else nc.sync
                queue.dma_start(out[j * J_TILE : (j + 1) * J_TILE, n_cols], results[:, j, n_cols])
